import numpy as np
import ml_dtypes


def mxq(x, axis, fmt="e4m3"):
    dtype, down = {"e4m3": (ml_dtypes.float8_e4m3fn, 7), "e5m2": (ml_dtypes.float8_e5m2, 14)}[fmt]
    v = np.moveaxis(np.asarray(x, np.float32).astype(ml_dtypes.bfloat16).astype(np.float64), axis, -1)
    blocks = v.reshape(v.shape[:-1] + (-1, 32))
    amax = np.abs(blocks).max(-1, keepdims=True)
    byte = np.maximum(np.where(amax > 0, np.frexp(amax)[1] - 1 + 127, 0) - down, 1)
    scale = np.exp2(byte - 127.0)
    codes = (blocks / scale).astype(np.float32).astype(dtype).astype(np.float64)
    return np.moveaxis((codes * scale).reshape(v.shape), -1, axis)


WIDE = False


def mx_kscale(k):
    if not WIDE:
        return np.ones(k)
    levels = np.array([10, -10, 5, -5, 0])
    if k % 512:
        return np.exp2(np.random.permutation(np.resize(levels, k // 32))).repeat(32)
    a = np.empty((k // 512, 16))
    for p in range(k // 512):
        a[p, :8] = np.random.permutation(np.resize(levels, 8))
        for g in range(8):
            far = levels[np.abs(levels - a[p, g]) >= 10]
            a[p, g + 8] = far[np.random.randint(len(far))]
    return np.exp2(a.ravel()).repeat(32)


def f64(x):
    return np.asarray(x).astype(np.float64)


def striped(idx):
    return np.tile(idx.reshape(-1, 16).T, (8, 1)).astype(np.uint16)


def unstriped(offs):
    return offs[:16].T.reshape(-1).astype(np.int64)


E2M1 = np.array([0.0, 0.5, 1.0, 1.5, 2.0, 3.0, 4.0, 6.0, -0.0, -0.5, -1.0, -1.5, -2.0, -3.0, -4.0, -6.0])


def pack_weight(w, fmt):
    k, n = w.shape
    w = f64(np.asarray(w, np.float32).astype(ml_dtypes.bfloat16)).reshape(k // 32, 32, n)
    amax = np.abs(w).max(1)
    if fmt == "e4m3":
        byte = np.frexp(amax)[1] - 1 + 127 - 7
    else:
        mant, ex = np.frexp(amax / 6.0)
        byte = np.where(mant > 0.5, ex, ex - 1) + 127
    byte = np.clip(np.where(amax > 0, byte, 1), 1, 254)
    scaled = (w * np.exp2(127.0 - byte)[:, None, :]).reshape(k, n).astype(np.float32)
    by_word = np.ascontiguousarray(scaled.reshape(k // 512, 128, 4, n).transpose(0, 1, 3, 2))
    if fmt == "e4m3":
        words = by_word.astype(ml_dtypes.float8_e4m3fn).view(np.uint8)
    else:
        c = by_word.astype(ml_dtypes.float4_e2m1fn).view(np.uint8) & 0xF
        words = (c[..., 0::2] | (c[..., 1::2] << 4)).reshape(k // 512, 128, 2 * n)
    return np.ascontiguousarray(words), np.ascontiguousarray(byte.astype(np.uint8).reshape(k // 512, 16, n))


def unpack_weight(words, scales, fmt):
    g, _, n = scales.shape
    words = np.ascontiguousarray(words).reshape(g, 128, n, -1)
    if fmt == "e4m3":
        vals = words.view(ml_dtypes.float8_e4m3fn).astype(np.float64)
    else:
        nib = np.empty((g, 128, n, 4), np.uint8)
        nib[..., 0::2] = words & 0xF
        nib[..., 1::2] = words >> 4
        vals = E2M1[nib]
    vals = vals * np.repeat(np.exp2(scales.astype(np.float64) - 127.0), 8, axis=1)[..., None]
    return vals.transpose(0, 1, 3, 2).reshape(g * 512, n)


def relu(v):
    return np.maximum(v, 0.0)


K, T, E, C, H, N = 1024, 1280, 4, 256, 1024, 128


def by_expert(wq, xq):
    return np.concatenate([wq[e].T @ xq[:, e * C:(e + 1) * C] for e in range(E)], axis=1)


def setup_inputs():
    n = np.random.standard_normal
    s = mx_kscale(K)[:, None]
    u = mx_kscale(H)
    w1 = [pack_weight(m, "e2m1") for m in n((E, K, H)) / np.sqrt(K) / s[None] * u[None, None, :]]
    w2 = [pack_weight(m, "e2m1") for m in n((E, H, N)) / np.sqrt(H) / u[None, :, None]]
    return {
        "xT": (n((K, T)) * s).astype(np.float32),
        "w1_words": np.stack([m[0] for m in w1]),
        "w1_scales": np.stack([m[1] for m in w1]),
        "w2_words": np.stack([m[0] for m in w2]),
        "w2_scales": np.stack([m[1] for m in w2]),
        "gate": np.tile(np.random.uniform(0.2, 1.0, E * C), (N, 1)).astype(np.float32),
        "offs": striped(np.random.permutation(T)[:E * C]),
        "dst": striped(np.random.permutation(T)[:E * C]),
    }


def reference(xT, w1_words, w1_scales, w2_words, w2_scales, gate, offs, dst):
    idx = unstriped(offs)
    w1 = np.stack([unpack_weight(w1_words[e], w1_scales[e], "e2m1") for e in range(E)])
    w2 = np.stack([unpack_weight(w2_words[e], w2_scales[e], "e2m1") for e in range(E)])
    xq = mxq(f64(xT)[:, idx], 0, "e4m3")
    h = relu(by_expert(w1, xq))
    y = by_expert(w2, mxq(h, 0, "e4m3"))
    out = np.zeros((N, T))
    out[:, unstriped(dst)] = f64(gate) * y
    return out

@@ -1,0 +1,213 @@
+from contextlib import ExitStack
+
+import concourse.mybir as mybir
+from concourse.masks import make_identity
+
+F32 = mybir.dt.float32
+BF16 = mybir.dt.bfloat16
+U32 = mybir.dt.uint32
+I32 = mybir.dt.int32
+U16 = mybir.dt.uint16
+U8 = mybir.dt.uint8
+E4M3 = mybir.dt.float8_e4m3fn_x4
+E2M1 = mybir.dt.float4_e2m1fn_x4
+COPY = mybir.ActivationFunctionType.Copy
+RELU = mybir.ActivationFunctionType.Relu
+MULT = mybir.AluOpType.mult
+
+P = 128
+K, T, E, C, H, N = 1024, 1280, 4, 256, 1024, 128
+SLOTS = E * C
+FLOPS = 2 * SLOTS * (K * H + H * N)
+
+CHUNKS = [
+    [(0, 512, 320), (512, 512, 224), (1024, 256, 160)],
+    [(0, 512, 0), (512, 512, 192), (1024, 256, 96)],
+]
+GATHERS = [
+    [(0, 256), (256, 512), (512, 768), (768, 1024)],
+    [(0, 160), (160, 320), (320, 512), (512, 672), (672, 832), (832, 1024)],
+]
+SCATTERS = [(0, 256), (256, 512), (512, 704), (704, 864), (864, 1024)]
+RELU_ON_VECTOR = (3, 4)
+TURN_ON_VECTOR = (6,)
+Y_ON_VECTOR = (2, 5)
+LAG1, LAG2, AHEAD = 1, 2, 32
+
+
+def tile_moe_two_mlp_relu_kernel(
+    tc, xT, w1_words, w1_scales, w2_words, w2_scales, gate, offs, dst, out
+):
+    nc = tc.nc
+    with ExitStack() as ctx:
+        lists = ctx.enter_context(tc.tile_pool(name="lists", bufs=1))
+        keep = ctx.enter_context(tc.tile_pool(name="keep", bufs=1))
+        work = ctx.enter_context(tc.tile_pool(name="work", bufs=3))
+        psum_a = ctx.enter_context(tc.psum_pool(name="psum_a", bufs=4))
+        psum_t = ctx.enter_context(tc.psum_pool(name="psum_t", bufs=2))
+        psum_y = ctx.enter_context(tc.psum_pool(name="psum_y", bufs=2))
+
+        offs_sb = lists.tile([P, SLOTS // 16], U16, name="offs_sb")
+        dst_sb = lists.tile([P, SLOTS // 16], U16, name="dst_sb")
+
+        x_raw = [
+            [keep.tile([P, 4, w], F32, name=f"x_raw{s}_{c}") for c, (t0, w, v) in enumerate(CHUNKS[s])]
+            for s in range(2)
+        ]
+        x_bf = [keep.tile([P, T, 4], BF16, name=f"x_bf{s}", align_bytes=64) for s in range(2)]
+        x_words = [keep.tile([P, T], U32, name=f"x_words{s}", align_bytes=64) for s in range(2)]
+        x_bytes = [keep.tile([P, T], U8, name=f"x_bytes{s}", align_bytes=64) for s in range(2)]
+        g_words = [keep.tile([P, SLOTS], U32, name=f"g_words{s}", align_bytes=64) for s in range(2)]
+        g_bytes = [keep.tile([P, SLOTS], U8, name=f"g_bytes{s}", align_bytes=64) for s in range(2)]
+        w1_sb = [keep.tile([P, 2, 2 * H], U8, name=f"w1_sb{e}", align_bytes=64) for e in range(E)]
+        w1_sc = keep.tile([P, 2 * E, H], U8, name="w1_sc", align_bytes=64)
+        w2_sb = keep.tile([P, 2 * E, 2 * N], U8, name="w2_sb", align_bytes=64)
+        w2_sc = keep.tile([P, 2 * E, N], U8, name="w2_sc", align_bytes=64)
+        gate_sb = keep.tile([P, SLOTS], F32, name="gate_sb")
+        y_sb = keep.tile([P, SLOTS], F32, name="y_sb")
+        out_sb = keep.tile([P, T], F32, name="out_sb")
+        ident = keep.tile([P, P], F32, name="ident")
+        dummy = keep.tile([P, 8], F32, name="dummy")
+
+        for s in range(2):
+            nc.gpsimd.memset(x_bytes[s][:], 0)
+        nc.gpsimd.memset(w1_sc[:].rearrange("p a i -> p (a i)").bitcast(I32), 0)
+        nc.gpsimd.memset(w2_sc[:].rearrange("p a i -> p (a i)").bitcast(I32), 0)
+        make_identity(nc, ident[:])
+        nc.vector.memset(dummy[:], 0.0)
+        nc.scalar.activation(dummy[:, 0:1], dummy[:, 1:2], RELU)
+        nc.vector.memset(out_sb[:], 0.0)
+
+        def load_x(s, c):
+            t0, w, v = CHUNKS[s][c]
+            src = xT[s * 512 : (s + 1) * 512, :].rearrange("(p j) t -> p j t", j=4)
+            nc.sync.dma_start(out=x_raw[s][c][:], in_=src[:, :, t0 : t0 + w])
+
+        def load_w1_scales(e0, e1):
+            for r in range(4):
+                nc.sync.dma_start(
+                    out=w1_sc[r:P:32, 2 * e0 : 2 * e1, :].bitcast(I32),
+                    in_=w1_scales[e0:e1, :, r::4, :].bitcast(I32).rearrange("e s q i -> q (e s) i"),
+                )
+
+        def load_w1(e):
+            nc.sync.dma_start(out=w1_sb[e][:].bitcast(I32), in_=w1_words[e].bitcast(I32).rearrange("s p b -> p s b"))
+
+        load_x(0, 0)
+        nc.sync.dma_start(offs_sb[:], offs)
+        load_x(0, 1)
+        load_x(0, 2)
+        load_x(1, 0)
+        load_x(1, 1)
+        load_x(1, 2)
+        load_w1_scales(0, 1)
+        load_w1(0)
+        load_w1_scales(1, 4)
+        load_w1(1)
+        for r in range(4):
+            nc.sync.dma_start(
+                out=w2_sc[r:P:32, :, :].bitcast(I32),
+                in_=w2_scales[:, :, r::4, :].bitcast(I32).rearrange("e s q i -> q (e s) i"),
+            )
+        nc.sync.dma_start(out=w2_sb[:].bitcast(I32), in_=w2_words.bitcast(I32).rearrange("e s p b -> p (e s) b"))
+        nc.sync.dma_start(dst_sb[:], dst)
+        nc.sync.dma_start(out=gate_sb[:], in_=gate)
+        load_w1(2)
+        load_w1(3)
+
+        for s in range(2):
+            for c, (t0, w, v) in enumerate(CHUNKS[s]):
+                raw = x_raw[s][c][:].rearrange("p j t -> p t j")
+                if v > 0:
+                    nc.vector.tensor_copy(x_bf[s][:, t0 : t0 + v, :], raw[:, 0:v, :])
+                if v < w:
+                    nc.scalar.activation(x_bf[s][:, t0 + v : t0 + w, :], raw[:, v:w, :], COPY)
+                nc.vector.quantize_mx(
+                    out=x_words[s][:, t0 : t0 + w].bitcast(E4M3),
+                    scales=x_bytes[s][:, t0 : t0 + w],
+                    in_=x_bf[s][:, t0 : t0 + w, :].rearrange("p t j -> p (t j)"),
+                )
+
+        def gather(s, a, b):
+            names = offs_sb[:, a // 16 : b // 16]
+            nc.vector.tensor_copy(g_words[s][:, a:b], x_words[s][:].indirect(names))
+            nc.vector.tensor_copy(g_bytes[s][:, a:b], x_bytes[s][:].indirect(names))
+
+        n_tiles = SLOTS // P
+        h_rows, h_turn, h_bf, h_words, h_bytes = {}, {}, {}, {}, {}
+
+        def layer1(i):
+            e = i // 2
+            cols = slice(i * P, (i + 1) * P)
+            h_rows[i] = work.tile([P, 2, 2, P, 2], BF16, name="h_rows", align_bytes=64)
+            for half in range(2):
+                acc = psum_a.tile([P, 512], F32, name="acc")
+                for s in range(2):
+                    nc.tensor.matmul_mx(
+                        out=acc[:],
+                        lhsT=g_words[s][:, cols].bitcast(E4M3),
+                        lhsT_scale=g_bytes[s][:, cols],
+                        rhs=w1_sb[e][:, s, half * 1024 : (half + 1) * 1024].bitcast(E2M1),
+                        rhs_scale=w1_sc[:, 2 * e + s, half * 512 : (half + 1) * 512],
+                        start=(s == 0),
+                        stop=(s == 1),
+                    )
+                pairs = acc[:].rearrange("r (p u e) -> r u p e", u=2, e=2)
+                if (2 * i + half) in RELU_ON_VECTOR:
+                    nc.vector.tensor_scalar_max(h_rows[i][:, half], pairs, 0.0)
+                else:
+                    nc.scalar.activation(h_rows[i][:, half], pairs, RELU)
+
+        def turn(i):
+            words = h_rows[i][:].rearrange("r h u p e -> r (h u p e)").bitcast(F32)
+            h_turn[i] = psum_t.tile([P, 512], F32, name="h_turn")
+            for k in range(4):
+                nc.tensor.transpose(h_turn[i][:, k * P : (k + 1) * P], words[:, k * P : (k + 1) * P], ident[:])
+            h_bf[i] = work.tile([P, 2 * P * 4], BF16, name="h_bf", align_bytes=64)
+            copy = nc.vector.tensor_copy if i in TURN_ON_VECTOR else nc.scalar.copy
+            copy(
+                h_bf[i][:].bitcast(F32).rearrange("p (h r u) -> p h r u", h=2, u=2),
+                h_turn[i][:].rearrange("p (h u r) -> p h r u", h=2, u=2),
+            )
+
+        def quantise_h(i):
+            h_words[i] = work.tile([P, 2 * P], U32, name="h_words", align_bytes=64)
+            h_bytes[i] = work.tile([P, 2 * P], U8, name="h_bytes", align_bytes=64)
+            nc.vector.quantize_mx(out=h_words[i][:].bitcast(E4M3), scales=h_bytes[i][:], in_=h_bf[i][:])
+
+        def layer2(i):
+            e = i // 2
+            y = psum_y.tile([P, P], F32, name="y")
+            for s in range(2):
+                nc.tensor.matmul_mx(
+                    out=y[:],
+                    lhsT=w2_sb[:, 2 * e + s, :].bitcast(E2M1),
+                    lhsT_scale=w2_sc[:, 2 * e + s, :],
+                    rhs=h_words[i][:, s * P : (s + 1) * P].bitcast(E4M3),
+                    rhs_scale=h_bytes[i][:, s * P : (s + 1) * P],
+                    start=(s == 0),
+                    stop=(s == 1),
+                )
+            copy = nc.vector.tensor_copy if i in Y_ON_VECTOR else nc.scalar.copy
+            copy(y_sb[:, i * P : (i + 1) * P], y[:])
+
+        scattered = 0
+        todo = [list(GATHERS[0]), list(GATHERS[1])]
+        for step in range(n_tiles + LAG2):
+            if step < n_tiles:
+                for s in range(2):
+                    while todo[s] and todo[s][0][0] < (step + 1) * P + AHEAD:
+                        gather(s, *todo[s].pop(0))
+                layer1(step)
+            if 0 <= step - LAG1 < n_tiles:
+                turn(step - LAG1)
+                quantise_h(step - LAG1)
+            if step >= LAG2:
+                layer2(step - LAG2)
+                while scattered < len(SCATTERS) and SCATTERS[scattered][1] <= (step - LAG2 + 1) * P:
+                    a, b = SCATTERS[scattered]
+                    nc.vector.tensor_tensor(
+                        out_sb[:].indirect(dst_sb[:, a // 16 : b // 16]), y_sb[:, a:b], gate_sb[:, a:b], MULT
+                    )
+                    scattered += 1
+        nc.sync.dma_start(out=out, in_=out_sb[:])

@@ -18,21 +18,20 @@ MULT = mybir.AluOpType.mult
 P = 128
 K, T, E, C, H, N = 1024, 1280, 4, 256, 1024, 128
 SLOTS = E * C
+N_TILES = SLOTS // P
 FLOPS = 2 * SLOTS * (K * H + H * N)
 
 CHUNKS = [
-    [(0, 512, 320), (512, 512, 224), (1024, 256, 160)],
-    [(0, 512, 0), (512, 512, 192), (1024, 256, 96)],
-]
-GATHERS = [
-    [(0, 256), (256, 512), (512, 768), (768, 1024)],
-    [(0, 160), (160, 320), (320, 512), (512, 672), (672, 832), (832, 1024)],
+    [(0, 768, 608), (768, 512, 128)],
+    [(0, 512, 0), (512, 512, 160), (1024, 256, 32)],
 ]
 SCATTERS = [(0, 256), (256, 512), (512, 704), (704, 864), (864, 1024)]
-RELU_ON_VECTOR = (3, 4)
-TURN_ON_VECTOR = (6,)
-Y_ON_VECTOR = (2, 5)
-LAG1, LAG2, AHEAD = 1, 2, 32
+RELU_ON_VECTOR = ()
+TURN_ON_VECTOR = (0,)
+Y_ON_VECTOR = (3, 5)
+PAIRED = (0,)
+LAG1, LAG2 = 1, 3
+GATHERS = [(0, 0, 0), (0, 0, 1), (0, 1, 0), (0, 1, 1), (1, 0, 2), (1, 1, 2), (3, 0, 3), (3, 1, 3)]
 
 
 def tile_moe_two_mlp_relu_kernel(
@@ -42,7 +41,7 @@ def tile_moe_two_mlp_relu_kernel(
     with ExitStack() as ctx:
         lists = ctx.enter_context(tc.tile_pool(name="lists", bufs=1))
         keep = ctx.enter_context(tc.tile_pool(name="keep", bufs=1))
-        work = ctx.enter_context(tc.tile_pool(name="work", bufs=3))
+        work = ctx.enter_context(tc.tile_pool(name="work", bufs=4))
         psum_a = ctx.enter_context(tc.psum_pool(name="psum_a", bufs=4))
         psum_t = ctx.enter_context(tc.psum_pool(name="psum_t", bufs=2))
         psum_y = ctx.enter_context(tc.psum_pool(name="psum_y", bufs=2))
@@ -50,32 +49,42 @@ def tile_moe_two_mlp_relu_kernel(
         offs_sb = lists.tile([P, SLOTS // 16], U16, name="offs_sb")
         dst_sb = lists.tile([P, SLOTS // 16], U16, name="dst_sb")
 
+        last = len(CHUNKS[1]) - 1
         x_raw = [
-            [keep.tile([P, 4, w], F32, name=f"x_raw{s}_{c}") for c, (t0, w, v) in enumerate(CHUNKS[s])]
+            [
+                keep.tile(
+                    [P, 4, w], F32, name=f"x_raw{s}_{c}", align_bytes=64,
+                    tag="late_bytes" if (s, c) == (1, last) else f"x_raw{s}_{c}",
+                )
+                for c, (t0, w, v) in enumerate(CHUNKS[s])
+            ]
             for s in range(2)
         ]
-        x_bf = [keep.tile([P, T, 4], BF16, name=f"x_bf{s}", align_bytes=64) for s in range(2)]
+        x_bf = [
+            keep.tile([P, T, 4], BF16, name=f"x_bf{s}", align_bytes=64, tag="late_words" if s == 1 else "x_bf0")
+            for s in range(2)
+        ]
         x_words = [keep.tile([P, T], U32, name=f"x_words{s}", align_bytes=64) for s in range(2)]
         x_bytes = [keep.tile([P, T], U8, name=f"x_bytes{s}", align_bytes=64) for s in range(2)]
-        g_words = [keep.tile([P, SLOTS], U32, name=f"g_words{s}", align_bytes=64) for s in range(2)]
-        g_bytes = [keep.tile([P, SLOTS], U8, name=f"g_bytes{s}", align_bytes=64) for s in range(2)]
         w1_sb = [keep.tile([P, 2, 2 * H], U8, name=f"w1_sb{e}", align_bytes=64) for e in range(E)]
-        w1_sc = keep.tile([P, 2 * E, H], U8, name="w1_sc", align_bytes=64)
-        w2_sb = keep.tile([P, 2 * E, 2 * N], U8, name="w2_sb", align_bytes=64)
-        w2_sc = keep.tile([P, 2 * E, N], U8, name="w2_sc", align_bytes=64)
+        w1_sc0 = keep.tile([P, 2, H], U8, name="w1_sc0", align_bytes=64)
+        w1_sc = keep.tile([P, 2 * (E - 1), H], U8, name="w1_sc", align_bytes=64)
+        w2_sb = keep.tile([P, E, 2, 2 * N], U8, name="w2_sb", align_bytes=64)
+        w2_sc = keep.tile([P, E, 2, N], U8, name="w2_sc", align_bytes=64)
         gate_sb = keep.tile([P, SLOTS], F32, name="gate_sb")
         y_sb = keep.tile([P, SLOTS], F32, name="y_sb")
         out_sb = keep.tile([P, T], F32, name="out_sb")
         ident = keep.tile([P, P], F32, name="ident")
         dummy = keep.tile([P, 8], F32, name="dummy")
 
+        nc.gpsimd.memset(w1_sc0[:].rearrange("p a i -> p (a i)").bitcast(I32), 0)
         for s in range(2):
-            nc.gpsimd.memset(x_bytes[s][:], 0)
-        nc.gpsimd.memset(w1_sc[:].rearrange("p a i -> p (a i)").bitcast(I32), 0)
-        nc.gpsimd.memset(w2_sc[:].rearrange("p a i -> p (a i)").bitcast(I32), 0)
+            nc.gpsimd.memset(x_bytes[s][:].bitcast(I32), 0)
+        nc.gpsimd.memset(w2_sc[:].rearrange("p a s i -> p (a s i)").bitcast(I32), 0)
         make_identity(nc, ident[:])
         nc.vector.memset(dummy[:], 0.0)
         nc.scalar.activation(dummy[:, 0:1], dummy[:, 1:2], RELU)
+        nc.vector.memset(w1_sc[:].rearrange("p a i -> p (a i)").bitcast(I32), 0)
         nc.vector.memset(out_sb[:], 0.0)
 
         def load_x(s, c):
@@ -83,123 +92,183 @@ def tile_moe_two_mlp_relu_kernel(
             src = xT[s * 512 : (s + 1) * 512, :].rearrange("(p j) t -> p j t", j=4)
             nc.sync.dma_start(out=x_raw[s][c][:], in_=src[:, :, t0 : t0 + w])
 
-        def load_w1_scales(e0, e1):
+        def load_w1_scales(tile, e0, e1):
             for r in range(4):
                 nc.sync.dma_start(
-                    out=w1_sc[r:P:32, 2 * e0 : 2 * e1, :].bitcast(I32),
+                    out=tile[r:P:32, :, :].bitcast(I32),
                     in_=w1_scales[e0:e1, :, r::4, :].bitcast(I32).rearrange("e s q i -> q (e s) i"),
                 )
 
         def load_w1(e):
             nc.sync.dma_start(out=w1_sb[e][:].bitcast(I32), in_=w1_words[e].bitcast(I32).rearrange("s p b -> p s b"))
 
+        def load_w1_pass(e, s):
+            nc.sync.dma_start(out=w1_sb[e][:, s, :].bitcast(I32), in_=w1_words[e, s].bitcast(I32))
+
+        def load_w2():
+            for s in range(2):
+                for v in range(2):
+                    nc.sync.dma_start(
+                        out=w2_sb[64 * s : 64 * s + 64, :, v, :].bitcast(I32),
+                        in_=w2_words[:, s, 64 * v : 64 * v + 64, :].bitcast(I32).rearrange("e q b -> q e b"),
+                    )
+
+        for q in range(4):
+            for v in range(2):
+                row = 8 * v + 4 * (q % 2)
+                nc.scalar.dma_start(
+                    out=w2_sc[32 * q : 32 * q + 4, :, v, :].bitcast(I32),
+                    in_=w2_scales[:, q // 2, row : row + 4, :].bitcast(I32).rearrange("e r n -> r e n"),
+                )
+
         load_x(0, 0)
         nc.sync.dma_start(offs_sb[:], offs)
+        nc.sync.dma_start(dst_sb[:], dst)
         load_x(0, 1)
-        load_x(0, 2)
         load_x(1, 0)
         load_x(1, 1)
         load_x(1, 2)
-        load_w1_scales(0, 1)
-        load_w1(0)
-        load_w1_scales(1, 4)
+        load_w1_scales(w1_sc0, 0, 1)
+        load_w1_pass(0, 0)
+        load_w1_pass(0, 1)
         load_w1(1)
-        for r in range(4):
-            nc.sync.dma_start(
-                out=w2_sc[r:P:32, :, :].bitcast(I32),
-                in_=w2_scales[:, :, r::4, :].bitcast(I32).rearrange("e s q i -> q (e s) i"),
-            )
-        nc.sync.dma_start(out=w2_sb[:].bitcast(I32), in_=w2_words.bitcast(I32).rearrange("e s p b -> p (e s) b"))
-        nc.sync.dma_start(dst_sb[:], dst)
-        nc.sync.dma_start(out=gate_sb[:], in_=gate)
+        load_w1_scales(w1_sc, 1, 4)
         load_w1(2)
+        load_w2()
+        nc.sync.dma_start(out=gate_sb[:], in_=gate)
         load_w1(3)
 
         for s in range(2):
             for c, (t0, w, v) in enumerate(CHUNKS[s]):
-                raw = x_raw[s][c][:].rearrange("p j t -> p t j")
-                if v > 0:
-                    nc.vector.tensor_copy(x_bf[s][:, t0 : t0 + v, :], raw[:, 0:v, :])
-                if v < w:
-                    nc.scalar.activation(x_bf[s][:, t0 + v : t0 + w, :], raw[:, v:w, :], COPY)
-                nc.vector.quantize_mx(
-                    out=x_words[s][:, t0 : t0 + w].bitcast(E4M3),
-                    scales=x_bytes[s][:, t0 : t0 + w],
-                    in_=x_bf[s][:, t0 : t0 + w, :].rearrange("p t j -> p (t j)"),
-                )
+                for engine, a, b in (("v", 0, v), ("s", v, w)):
+                    if a < b:
+                        raw = x_raw[s][c][:, :, a:b].rearrange("p j (c i) -> p c j i", i=4)
+                        grouped = x_bf[s][:, t0 + a : t0 + b, :].rearrange("p (c i) j -> p c j i", i=4)
+                        if engine == "v":
+                            nc.vector.tensor_copy(grouped, raw)
+                        else:
+                            nc.scalar.activation(grouped, raw, COPY)
+                done = 0
+                for width in (512, 256, 128):
+                    while w - done >= width:
+                        tokens = slice(t0 + done, t0 + done + width)
+                        nc.vector.quantize_mx(
+                            out=x_words[s][:, tokens].bitcast(E4M3),
+                            scales=x_bytes[s][:, tokens],
+                            in_=x_bf[s][:, tokens, :].rearrange("p t j -> p (t j)"),
+                        )
+                        done += width
 
-        def gather(s, a, b):
-            names = offs_sb[:, a // 16 : b // 16]
-            nc.vector.tensor_copy(g_words[s][:, a:b], x_words[s][:].indirect(names))
-            nc.vector.tensor_copy(g_bytes[s][:, a:b], x_bytes[s][:].indirect(names))
+        g_words, g_bytes = {}, {}
 
-        n_tiles = SLOTS // P
+        def picked(pairs, words_tag, bytes_tag):
+            words = keep.tile([P, len(pairs), C], U32, name="g_words_" + words_tag, tag=words_tag, align_bytes=64)
+            codes = keep.tile([P, len(pairs), C], U8, name="g_bytes_" + words_tag, tag=bytes_tag, align_bytes=64)
+            for j, key in enumerate(pairs):
+                g_words[key], g_bytes[key] = words[:, j, :], codes[:, j, :]
+
+        picked([(0, 0), (0, 1)], "words_a", "bytes_a")
+        picked([(1, 0), (1, 1), (1, 2)], "words_b", "bytes_b")
+        picked([(0, 2)], "late_words", "late_bytes")
+
+        def gather(s, e):
+            names = offs_sb[:, e * C // 16 : (e + 1) * C // 16]
+            nc.vector.tensor_copy(g_words[s, e], x_words[s][:].indirect(names))
+            nc.vector.tensor_copy(g_bytes[s, e], x_bytes[s][:].indirect(names))
+
         h_rows, h_turn, h_bf, h_words, h_bytes = {}, {}, {}, {}, {}
 
         def layer1(i):
             e = i // 2
-            cols = slice(i * P, (i + 1) * P)
-            h_rows[i] = work.tile([P, 2, 2, P, 2], BF16, name="h_rows", align_bytes=64)
+            cols = slice((i % 2) * P, (i % 2 + 1) * P)
+            scales = w1_sc0[:, 0:2, :] if e == 0 else w1_sc[:, 2 * e - 2 : 2 * e, :]
+            h_rows[i] = keep.tile([P, 2, 2, 2, 64, 2], BF16, name=f"h_rows{i}", tag=f"h_rows{i}", align_bytes=64)
             for half in range(2):
                 acc = psum_a.tile([P, 512], F32, name="acc")
                 for s in range(2):
                     nc.tensor.matmul_mx(
                         out=acc[:],
-                        lhsT=g_words[s][:, cols].bitcast(E4M3),
-                        lhsT_scale=g_bytes[s][:, cols],
+                        lhsT=g_words[s, e][:, cols].bitcast(E4M3),
+                        lhsT_scale=g_bytes[s, e][:, cols],
                         rhs=w1_sb[e][:, s, half * 1024 : (half + 1) * 1024].bitcast(E2M1),
-                        rhs_scale=w1_sc[:, 2 * e + s, half * 512 : (half + 1) * 512],
+                        rhs_scale=scales[:, s, half * 512 : (half + 1) * 512],
                         start=(s == 0),
                         stop=(s == 1),
                     )
-                pairs = acc[:].rearrange("r (p u e) -> r u p e", u=2, e=2)
+                pairs = acc[:].rearrange("r (v p u e) -> r u v p e", v=2, u=2, e=2)
                 if (2 * i + half) in RELU_ON_VECTOR:
-                    nc.vector.tensor_scalar_max(h_rows[i][:, half], pairs, 0.0)
+                    nc.vector.tensor_scalar_max(h_rows[i][:, :, :, half], pairs, 0.0)
                 else:
-                    nc.scalar.activation(h_rows[i][:, half], pairs, RELU)
+                    nc.scalar.activation(h_rows[i][:, :, :, half], pairs, RELU)
 
         def turn(i):
-            words = h_rows[i][:].rearrange("r h u p e -> r (h u p e)").bitcast(F32)
+            words = h_rows[i][:].rearrange("r u v h p e -> r (u v h p e)").bitcast(F32)
             h_turn[i] = psum_t.tile([P, 512], F32, name="h_turn")
-            for k in range(4):
-                nc.tensor.transpose(h_turn[i][:, k * P : (k + 1) * P], words[:, k * P : (k + 1) * P], ident[:])
-            h_bf[i] = work.tile([P, 2 * P * 4], BF16, name="h_bf", align_bytes=64)
+            for u in range(2):
+                for v in range(2):
+                    to, k = 2 * v + u, 2 * u + v
+                    nc.tensor.transpose(h_turn[i][:, to * P : (to + 1) * P], words[:, k * P : (k + 1) * P], ident[:])
+            if i // 2 in PAIRED:
+                if i % 2 == 0:
+                    pair = keep.tile([P, 2, 2 * P * 4], BF16, name=f"h_bf2_{i}", tag="h_bf2" if i == 0 else f"h_bf2_{i}", align_bytes=64)
+                    h_bf[i], h_bf[i + 1] = pair[:, 0, :], pair[:, 1, :]
+                    h_bf[i // 2, "pair"] = pair
+            else:
+                h_bf[i] = keep.tile([P, 2 * P * 4], BF16, name=f"h_bf{i}", align_bytes=64)[:]
             copy = nc.vector.tensor_copy if i in TURN_ON_VECTOR else nc.scalar.copy
             copy(
-                h_bf[i][:].bitcast(F32).rearrange("p (h r u) -> p h r u", h=2, u=2),
-                h_turn[i][:].rearrange("p (h u r) -> p h r u", h=2, u=2),
+                h_bf[i].bitcast(F32).rearrange("p (v r u) -> p v r u", v=2, u=2),
+                h_turn[i][:].rearrange("p (v u r) -> p v r u", v=2, u=2),
             )
 
         def quantise_h(i):
-            h_words[i] = work.tile([P, 2 * P], U32, name="h_words", align_bytes=64)
-            h_bytes[i] = work.tile([P, 2 * P], U8, name="h_bytes", align_bytes=64)
-            nc.vector.quantize_mx(out=h_words[i][:].bitcast(E4M3), scales=h_bytes[i][:], in_=h_bf[i][:])
+            if i // 2 in PAIRED:
+                if i % 2 == 1:
+                    words = work.tile([P, 2, 2 * P], U32, name="h_words2", align_bytes=64)
+                    bytes_ = work.tile([P, 2, 2 * P], U8, name="h_bytes2", align_bytes=64)
+                    nc.vector.quantize_mx(
+                        out=words[:].rearrange("p a b -> p (a b)").bitcast(E4M3),
+                        scales=bytes_[:].rearrange("p a b -> p (a b)"),
+                        in_=h_bf[i // 2, "pair"][:].rearrange("p a b -> p (a b)"),
+                    )
+                    for j in range(2):
+                        h_words[i - 1 + j], h_bytes[i - 1 + j] = words[:, j, :], bytes_[:, j, :]
+            else:
+                words = work.tile([P, 2 * P], U32, name="h_words", align_bytes=64)
+                bytes_ = work.tile([P, 2 * P], U8, name="h_bytes", align_bytes=64)
+                nc.vector.quantize_mx(out=words[:].bitcast(E4M3), scales=bytes_[:], in_=h_bf[i])
+                h_words[i], h_bytes[i] = words[:], bytes_[:]
 
         def layer2(i):
             e = i // 2
-            y = psum_y.tile([P, P], F32, name="y")
-            for s in range(2):
-                nc.tensor.matmul_mx(
-                    out=y[:],
-                    lhsT=w2_sb[:, 2 * e + s, :].bitcast(E2M1),
-                    lhsT_scale=w2_sc[:, 2 * e + s, :],
-                    rhs=h_words[i][:, s * P : (s + 1) * P].bitcast(E4M3),
-                    rhs_scale=h_bytes[i][:, s * P : (s + 1) * P],
-                    start=(s == 0),
-                    stop=(s == 1),
-                )
+            if e in PAIRED and i % 2 == 0:
+                return
+            tiles = (i - 1, i) if e in PAIRED else (i,)
+            y = psum_y.tile([P, 2 * P], F32, name="y")
+            for j, k in enumerate(tiles):
+                for s in range(2):
+                    nc.tensor.matmul_mx(
+                        out=y[:, j * P : (j + 1) * P],
+                        lhsT=w2_sb[:, e, s, :].bitcast(E2M1),
+                        lhsT_scale=w2_sc[:, e, s, :],
+                        rhs=h_words[k][:, s * P : (s + 1) * P].bitcast(E4M3),
+                        rhs_scale=h_bytes[k][:, s * P : (s + 1) * P],
+                        start=(s == 0),
+                        stop=(s == 1),
+                    )
             copy = nc.vector.tensor_copy if i in Y_ON_VECTOR else nc.scalar.copy
-            copy(y_sb[:, i * P : (i + 1) * P], y[:])
+            copy(y_sb[:, tiles[0] * P : (i + 1) * P], y[:, 0 : len(tiles) * P])
 
         scattered = 0
-        todo = [list(GATHERS[0]), list(GATHERS[1])]
-        for step in range(n_tiles + LAG2):
-            if step < n_tiles:
-                for s in range(2):
-                    while todo[s] and todo[s][0][0] < (step + 1) * P + AHEAD:
-                        gather(s, *todo[s].pop(0))
+        for step in range(N_TILES + LAG2):
+            for at, s, e in GATHERS:
+                if at == step:
+                    if (s, e) == (0, 3):
+                        picked([(0, 3), (1, 3)], "h_bf2", "h_rows1")
+                    gather(s, e)
+            if step < N_TILES:
                 layer1(step)
-            if 0 <= step - LAG1 < n_tiles:
+            if 0 <= step - LAG1 < N_TILES:
                 turn(step - LAG1)
                 quantise_h(step - LAG1)
             if step >= LAG2:

@@ -22,16 +22,16 @@ N_TILES = SLOTS // P
 FLOPS = 2 * SLOTS * (K * H + H * N)
 
 CHUNKS = [
-    [(0, 768, 608), (768, 512, 128)],
-    [(0, 512, 0), (512, 512, 160), (1024, 256, 32)],
+    [(0, 512, 352), (512, 512, 224), (1024, 256, 128)],
+    [(0, 512, 0), (512, 512, 160), (1024, 256, 96)],
 ]
-SCATTERS = [(0, 256), (256, 512), (512, 704), (704, 864), (864, 1024)]
+SCATTERS = [(0, 192), (192, 352), (352, 512), (512, 672), (672, 832), (832, 1024)]
 RELU_ON_VECTOR = ()
-TURN_ON_VECTOR = (0,)
-Y_ON_VECTOR = (3, 5)
-PAIRED = (0,)
-LAG1, LAG2 = 1, 3
-GATHERS = [(0, 0, 0), (0, 0, 1), (0, 1, 0), (0, 1, 1), (1, 0, 2), (1, 1, 2), (3, 0, 3), (3, 1, 3)]
+TURN_ON_VECTOR = (2, 3)
+Y_ON_VECTOR = (1,)
+PAIRED = ()
+LAG1, LAG2 = 2, 4
+GATHERS = [(0, 0, 0), (0, 0, 1), (0, 1, 0), (0, 1, 1), (0, 0, 2), (0, 1, 2), (0, 0, 3), (0, 1, 3)]
 
 
 def tile_moe_two_mlp_relu_kernel(
@@ -116,7 +116,7 @@ def tile_moe_two_mlp_relu_kernel(
         for q in range(4):
             for v in range(2):
                 row = 8 * v + 4 * (q % 2)
-                nc.scalar.dma_start(
+                nc.gpsimd.dma_start(
                     out=w2_sc[32 * q : 32 * q + 4, :, v, :].bitcast(I32),
                     in_=w2_scales[:, q // 2, row : row + 4, :].bitcast(I32).rearrange("e r n -> r e n"),
                 )
@@ -125,6 +125,7 @@ def tile_moe_two_mlp_relu_kernel(
         nc.sync.dma_start(offs_sb[:], offs)
         nc.sync.dma_start(dst_sb[:], dst)
         load_x(0, 1)
+        load_x(0, 2)
         load_x(1, 0)
         load_x(1, 1)
         load_x(1, 2)
@@ -134,9 +135,9 @@ def tile_moe_two_mlp_relu_kernel(
         load_w1(1)
         load_w1_scales(w1_sc, 1, 4)
         load_w1(2)
-        load_w2()
-        nc.sync.dma_start(out=gate_sb[:], in_=gate)
         load_w1(3)
+        nc.sync.dma_start(out=gate_sb[:], in_=gate)
+        load_w2()
 
         for s in range(2):
             for c, (t0, w, v) in enumerate(CHUNKS[s]):
@@ -168,8 +169,8 @@ def tile_moe_two_mlp_relu_kernel(
                 g_words[key], g_bytes[key] = words[:, j, :], codes[:, j, :]
 
         picked([(0, 0), (0, 1)], "words_a", "bytes_a")
-        picked([(1, 0), (1, 1), (1, 2)], "words_b", "bytes_b")
-        picked([(0, 2)], "late_words", "late_bytes")
+        picked([(1, 0), (1, 1), (1, 2), (1, 3)], "words_b", "bytes_b")
+        picked([(0, 2), (0, 3)], "late_words", "late_bytes")
 
         def gather(s, e):
             names = offs_sb[:, e * C // 16 : (e + 1) * C // 16]
@@ -263,8 +264,6 @@ def tile_moe_two_mlp_relu_kernel(
         for step in range(N_TILES + LAG2):
             for at, s, e in GATHERS:
                 if at == step:
-                    if (s, e) == (0, 3):
-                        picked([(0, 3), (1, 3)], "h_bf2", "h_rows1")
                     gather(s, e)
             if step < N_TILES:
                 layer1(step)

from contextlib import ExitStack

import concourse.mybir as mybir
from concourse.masks import make_identity

F32 = mybir.dt.float32
BF16 = mybir.dt.bfloat16
U32 = mybir.dt.uint32
I32 = mybir.dt.int32
U16 = mybir.dt.uint16
U8 = mybir.dt.uint8
E4M3 = mybir.dt.float8_e4m3fn_x4
E2M1 = mybir.dt.float4_e2m1fn_x4
COPY = mybir.ActivationFunctionType.Copy
RELU = mybir.ActivationFunctionType.Relu
MULT = mybir.AluOpType.mult

P = 128
K, T, E, C, H, N = 1024, 1280, 4, 256, 1024, 128
SLOTS = E * C
N_TILES = SLOTS // P
FLOPS = 2 * SLOTS * (K * H + H * N)

CHUNKS = [
    [(0, 512, 352), (512, 512, 224), (1024, 256, 128)],
    [(0, 512, 0), (512, 512, 160), (1024, 256, 96)],
]
SCATTERS = [(0, 192), (192, 352), (352, 512), (512, 672), (672, 832), (832, 1024)]
RELU_ON_VECTOR = ()
TURN_ON_VECTOR = (2, 3)
Y_ON_VECTOR = (1,)
PAIRED = ()
LAG1, LAG2 = 2, 4
GATHERS = [(0, 0, 0), (0, 0, 1), (0, 1, 0), (0, 1, 1), (0, 0, 2), (0, 1, 2), (0, 0, 3), (0, 1, 3)]


def tile_moe_two_mlp_relu_kernel(
    tc, xT, w1_words, w1_scales, w2_words, w2_scales, gate, offs, dst, out
):
    nc = tc.nc
    with ExitStack() as ctx:
        lists = ctx.enter_context(tc.tile_pool(name="lists", bufs=1))
        keep = ctx.enter_context(tc.tile_pool(name="keep", bufs=1))
        work = ctx.enter_context(tc.tile_pool(name="work", bufs=4))
        psum_a = ctx.enter_context(tc.psum_pool(name="psum_a", bufs=4))
        psum_t = ctx.enter_context(tc.psum_pool(name="psum_t", bufs=2))
        psum_y = ctx.enter_context(tc.psum_pool(name="psum_y", bufs=2))

        offs_sb = lists.tile([P, SLOTS // 16], U16, name="offs_sb")
        dst_sb = lists.tile([P, SLOTS // 16], U16, name="dst_sb")

        last = len(CHUNKS[1]) - 1
        x_raw = [
            [
                keep.tile(
                    [P, 4, w], F32, name=f"x_raw{s}_{c}", align_bytes=64,
                    tag="late_bytes" if (s, c) == (1, last) else f"x_raw{s}_{c}",
                )
                for c, (t0, w, v) in enumerate(CHUNKS[s])
            ]
            for s in range(2)
        ]
        x_bf = [
            keep.tile([P, T, 4], BF16, name=f"x_bf{s}", align_bytes=64, tag="late_words" if s == 1 else "x_bf0")
            for s in range(2)
        ]
        x_words = [keep.tile([P, T], U32, name=f"x_words{s}", align_bytes=64) for s in range(2)]
        x_bytes = [keep.tile([P, T], U8, name=f"x_bytes{s}", align_bytes=64) for s in range(2)]
        w1_sb = [keep.tile([P, 2, 2 * H], U8, name=f"w1_sb{e}", align_bytes=64) for e in range(E)]
        w1_sc0 = keep.tile([P, 2, H], U8, name="w1_sc0", align_bytes=64)
        w1_sc = keep.tile([P, 2 * (E - 1), H], U8, name="w1_sc", align_bytes=64)
        w2_sb = keep.tile([P, E, 2, 2 * N], U8, name="w2_sb", align_bytes=64)
        w2_sc = keep.tile([P, E, 2, N], U8, name="w2_sc", align_bytes=64)
        gate_sb = keep.tile([P, SLOTS], F32, name="gate_sb")
        y_sb = keep.tile([P, SLOTS], F32, name="y_sb")
        out_sb = keep.tile([P, T], F32, name="out_sb")
        ident = keep.tile([P, P], F32, name="ident")
        dummy = keep.tile([P, 8], F32, name="dummy")

        nc.gpsimd.memset(w1_sc0[:].rearrange("p a i -> p (a i)").bitcast(I32), 0)
        for s in range(2):
            nc.gpsimd.memset(x_bytes[s][:].bitcast(I32), 0)
        nc.gpsimd.memset(w2_sc[:].rearrange("p a s i -> p (a s i)").bitcast(I32), 0)
        make_identity(nc, ident[:])
        nc.vector.memset(dummy[:], 0.0)
        nc.scalar.activation(dummy[:, 0:1], dummy[:, 1:2], RELU)
        nc.vector.memset(w1_sc[:].rearrange("p a i -> p (a i)").bitcast(I32), 0)
        nc.vector.memset(out_sb[:], 0.0)

        def load_x(s, c):
            t0, w, v = CHUNKS[s][c]
            src = xT[s * 512 : (s + 1) * 512, :].rearrange("(p j) t -> p j t", j=4)
            nc.sync.dma_start(out=x_raw[s][c][:], in_=src[:, :, t0 : t0 + w])

        def load_w1_scales(tile, e0, e1):
            for r in range(4):
                nc.sync.dma_start(
                    out=tile[r:P:32, :, :].bitcast(I32),
                    in_=w1_scales[e0:e1, :, r::4, :].bitcast(I32).rearrange("e s q i -> q (e s) i"),
                )

        def load_w1(e):
            nc.sync.dma_start(out=w1_sb[e][:].bitcast(I32), in_=w1_words[e].bitcast(I32).rearrange("s p b -> p s b"))

        def load_w1_pass(e, s):
            nc.sync.dma_start(out=w1_sb[e][:, s, :].bitcast(I32), in_=w1_words[e, s].bitcast(I32))

        def load_w2():
            for s in range(2):
                for v in range(2):
                    nc.sync.dma_start(
                        out=w2_sb[64 * s : 64 * s + 64, :, v, :].bitcast(I32),
                        in_=w2_words[:, s, 64 * v : 64 * v + 64, :].bitcast(I32).rearrange("e q b -> q e b"),
                    )

        for q in range(4):
            for v in range(2):
                row = 8 * v + 4 * (q % 2)
                nc.gpsimd.dma_start(
                    out=w2_sc[32 * q : 32 * q + 4, :, v, :].bitcast(I32),
                    in_=w2_scales[:, q // 2, row : row + 4, :].bitcast(I32).rearrange("e r n -> r e n"),
                )

        load_x(0, 0)
        nc.sync.dma_start(offs_sb[:], offs)
        nc.sync.dma_start(dst_sb[:], dst)
        load_x(0, 1)
        load_x(0, 2)
        load_x(1, 0)
        load_x(1, 1)
        load_x(1, 2)
        load_w1_scales(w1_sc0, 0, 1)
        load_w1_pass(0, 0)
        load_w1_pass(0, 1)
        load_w1(1)
        load_w1_scales(w1_sc, 1, 4)
        load_w1(2)
        load_w1(3)
        nc.sync.dma_start(out=gate_sb[:], in_=gate)
        load_w2()

        for s in range(2):
            for c, (t0, w, v) in enumerate(CHUNKS[s]):
                for engine, a, b in (("v", 0, v), ("s", v, w)):
                    if a < b:
                        raw = x_raw[s][c][:, :, a:b].rearrange("p j (c i) -> p c j i", i=4)
                        grouped = x_bf[s][:, t0 + a : t0 + b, :].rearrange("p (c i) j -> p c j i", i=4)
                        if engine == "v":
                            nc.vector.tensor_copy(grouped, raw)
                        else:
                            nc.scalar.activation(grouped, raw, COPY)
                done = 0
                for width in (512, 256, 128):
                    while w - done >= width:
                        tokens = slice(t0 + done, t0 + done + width)
                        nc.vector.quantize_mx(
                            out=x_words[s][:, tokens].bitcast(E4M3),
                            scales=x_bytes[s][:, tokens],
                            in_=x_bf[s][:, tokens, :].rearrange("p t j -> p (t j)"),
                        )
                        done += width

        g_words, g_bytes = {}, {}

        def picked(pairs, words_tag, bytes_tag):
            words = keep.tile([P, len(pairs), C], U32, name="g_words_" + words_tag, tag=words_tag, align_bytes=64)
            codes = keep.tile([P, len(pairs), C], U8, name="g_bytes_" + words_tag, tag=bytes_tag, align_bytes=64)
            for j, key in enumerate(pairs):
                g_words[key], g_bytes[key] = words[:, j, :], codes[:, j, :]

        picked([(0, 0), (0, 1)], "words_a", "bytes_a")
        picked([(1, 0), (1, 1), (1, 2), (1, 3)], "words_b", "bytes_b")
        picked([(0, 2), (0, 3)], "late_words", "late_bytes")

        def gather(s, e):
            names = offs_sb[:, e * C // 16 : (e + 1) * C // 16]
            nc.vector.tensor_copy(g_words[s, e], x_words[s][:].indirect(names))
            nc.vector.tensor_copy(g_bytes[s, e], x_bytes[s][:].indirect(names))

        h_rows, h_turn, h_bf, h_words, h_bytes = {}, {}, {}, {}, {}

        def layer1(i):
            e = i // 2
            cols = slice((i % 2) * P, (i % 2 + 1) * P)
            scales = w1_sc0[:, 0:2, :] if e == 0 else w1_sc[:, 2 * e - 2 : 2 * e, :]
            h_rows[i] = keep.tile([P, 2, 2, 2, 64, 2], BF16, name=f"h_rows{i}", tag=f"h_rows{i}", align_bytes=64)
            for half in range(2):
                acc = psum_a.tile([P, 512], F32, name="acc")
                for s in range(2):
                    nc.tensor.matmul_mx(
                        out=acc[:],
                        lhsT=g_words[s, e][:, cols].bitcast(E4M3),
                        lhsT_scale=g_bytes[s, e][:, cols],
                        rhs=w1_sb[e][:, s, half * 1024 : (half + 1) * 1024].bitcast(E2M1),
                        rhs_scale=scales[:, s, half * 512 : (half + 1) * 512],
                        start=(s == 0),
                        stop=(s == 1),
                    )
                pairs = acc[:].rearrange("r (v p u e) -> r u v p e", v=2, u=2, e=2)
                if (2 * i + half) in RELU_ON_VECTOR:
                    nc.vector.tensor_scalar_max(h_rows[i][:, :, :, half], pairs, 0.0)
                else:
                    nc.scalar.activation(h_rows[i][:, :, :, half], pairs, RELU)

        def turn(i):
            words = h_rows[i][:].rearrange("r u v h p e -> r (u v h p e)").bitcast(F32)
            h_turn[i] = psum_t.tile([P, 512], F32, name="h_turn")
            for u in range(2):
                for v in range(2):
                    to, k = 2 * v + u, 2 * u + v
                    nc.tensor.transpose(h_turn[i][:, to * P : (to + 1) * P], words[:, k * P : (k + 1) * P], ident[:])
            if i // 2 in PAIRED:
                if i % 2 == 0:
                    pair = keep.tile([P, 2, 2 * P * 4], BF16, name=f"h_bf2_{i}", tag="h_bf2" if i == 0 else f"h_bf2_{i}", align_bytes=64)
                    h_bf[i], h_bf[i + 1] = pair[:, 0, :], pair[:, 1, :]
                    h_bf[i // 2, "pair"] = pair
            else:
                h_bf[i] = keep.tile([P, 2 * P * 4], BF16, name=f"h_bf{i}", align_bytes=64)[:]
            copy = nc.vector.tensor_copy if i in TURN_ON_VECTOR else nc.scalar.copy
            copy(
                h_bf[i].bitcast(F32).rearrange("p (v r u) -> p v r u", v=2, u=2),
                h_turn[i][:].rearrange("p (v u r) -> p v r u", v=2, u=2),
            )

        def quantise_h(i):
            if i // 2 in PAIRED:
                if i % 2 == 1:
                    words = work.tile([P, 2, 2 * P], U32, name="h_words2", align_bytes=64)
                    bytes_ = work.tile([P, 2, 2 * P], U8, name="h_bytes2", align_bytes=64)
                    nc.vector.quantize_mx(
                        out=words[:].rearrange("p a b -> p (a b)").bitcast(E4M3),
                        scales=bytes_[:].rearrange("p a b -> p (a b)"),
                        in_=h_bf[i // 2, "pair"][:].rearrange("p a b -> p (a b)"),
                    )
                    for j in range(2):
                        h_words[i - 1 + j], h_bytes[i - 1 + j] = words[:, j, :], bytes_[:, j, :]
            else:
                words = work.tile([P, 2 * P], U32, name="h_words", align_bytes=64)
                bytes_ = work.tile([P, 2 * P], U8, name="h_bytes", align_bytes=64)
                nc.vector.quantize_mx(out=words[:].bitcast(E4M3), scales=bytes_[:], in_=h_bf[i])
                h_words[i], h_bytes[i] = words[:], bytes_[:]

        def layer2(i):
            e = i // 2
            if e in PAIRED and i % 2 == 0:
                return
            tiles = (i - 1, i) if e in PAIRED else (i,)
            y = psum_y.tile([P, 2 * P], F32, name="y")
            for j, k in enumerate(tiles):
                for s in range(2):
                    nc.tensor.matmul_mx(
                        out=y[:, j * P : (j + 1) * P],
                        lhsT=w2_sb[:, e, s, :].bitcast(E2M1),
                        lhsT_scale=w2_sc[:, e, s, :],
                        rhs=h_words[k][:, s * P : (s + 1) * P].bitcast(E4M3),
                        rhs_scale=h_bytes[k][:, s * P : (s + 1) * P],
                        start=(s == 0),
                        stop=(s == 1),
                    )
            copy = nc.vector.tensor_copy if i in Y_ON_VECTOR else nc.scalar.copy
            copy(y_sb[:, tiles[0] * P : (i + 1) * P], y[:, 0 : len(tiles) * P])

        scattered = 0
        for step in range(N_TILES + LAG2):
            for at, s, e in GATHERS:
                if at == step:
                    gather(s, e)
            if step < N_TILES:
                layer1(step)
            if 0 <= step - LAG1 < N_TILES:
                turn(step - LAG1)
                quantise_h(step - LAG1)
            if step >= LAG2:
                layer2(step - LAG2)
                while scattered < len(SCATTERS) and SCATTERS[scattered][1] <= (step - LAG2 + 1) * P:
                    a, b = SCATTERS[scattered]
                    nc.vector.tensor_tensor(
                        out_sb[:].indirect(dst_sb[:, a // 16 : b // 16]), y_sb[:, a:b], gate_sb[:, a:b], MULT
                    )
                    scattered += 1
        nc.sync.dma_start(out=out, in_=out_sb[:])
